import numpy as np
import ml_dtypes


def mxq(x, axis, fmt="e4m3"):
    dtype, down = {"e4m3": (ml_dtypes.float8_e4m3fn, 7), "e5m2": (ml_dtypes.float8_e5m2, 14)}[fmt]
    v = np.moveaxis(np.asarray(x, np.float32).astype(ml_dtypes.bfloat16).astype(np.float64), axis, -1)
    blocks = v.reshape(v.shape[:-1] + (-1, 32))
    amax = np.abs(blocks).max(-1, keepdims=True)
    byte = np.maximum(np.where(amax > 0, np.frexp(amax)[1] - 1 + 127, 0) - down, 1)
    scale = np.exp2(byte - 127.0)
    codes = (blocks / scale).astype(np.float32).astype(dtype).astype(np.float64)
    return np.moveaxis((codes * scale).reshape(v.shape), -1, axis)


WIDE = False


def mx_kscale(k):
    if not WIDE:
        return np.ones(k)
    levels = np.array([10, -10, 5, -5, 0])
    if k % 512:
        return np.exp2(np.random.permutation(np.resize(levels, k // 32))).repeat(32)
    a = np.empty((k // 512, 16))
    for p in range(k // 512):
        a[p, :8] = np.random.permutation(np.resize(levels, 8))
        for g in range(8):
            far = levels[np.abs(levels - a[p, g]) >= 10]
            a[p, g + 8] = far[np.random.randint(len(far))]
    return np.exp2(a.ravel()).repeat(32)


BF16 = ml_dtypes.bfloat16


def bf(x):
    return np.asarray(x, np.float32).astype(BF16)


def f64(x):
    return np.asarray(x).astype(np.float64)


M, N, D = 1024, 1024, 1024


def draw0():
    s, t = mx_kscale(N), mx_kscale(D)
    return {
        "p": bf(np.random.standard_normal((M, N)) / np.sqrt(N) * s[None, :]),
        "h": bf(np.random.standard_normal((N, D)) / s[:, None]),
        "h0": bf(np.random.standard_normal((M, D))),
        "g": bf((1.0 + 0.1 * np.random.standard_normal(D)) * t),
        "w": bf(np.random.standard_normal((D, D)) / np.sqrt(D) / t[:, None]),
    }


def core(p, h, h0, g, w):
    u = mxq(f64(p), 1, "e4m3") @ mxq(f64(h), 0, "e4m3")
    s = 0.7 * u + 0.3 * f64(h0)
    sg = s * f64(g)[None, :]
    t = mxq(sg, 1, "e4m3") @ mxq(f64(w), 0, "e4m3")
    return np.maximum(0.5 * s + 0.5 * t, 0.0)


def e4m3fn_bytes(y):
    return np.clip(np.asarray(y, np.float64), -448.0, 448.0).astype(np.float32).astype(ml_dtypes.float8_e4m3fn).view(np.uint8)


def e4m3fn_values(b):
    return np.asarray(b, np.uint8).view(ml_dtypes.float8_e4m3fn).astype(np.float64)


def setup_inputs():
    d = draw0()
    x0 = np.asarray(d['w']).astype(np.float64)
    s = (np.max(np.abs(x0), axis=(1,), keepdims=True) / 448.0).astype(np.float32)
    out = {}
    for k, v in d.items():
        if k == 'w':
            out['w_bytes'] = e4m3fn_bytes(x0 / s.astype(np.float64))
            out['w_scale'] = s
        else:
            out[k] = v
    return out


def reference(p, h, h0, g, w_bytes, w_scale):
    return core(p, h, h0, g, e4m3fn_values(w_bytes) * w_scale.astype(np.float64))

@@ -1,0 +1,293 @@
+from contextlib import ExitStack
+
+import concourse.mybir as mybir
+from concourse.masks import make_identity
+
+N = 1024
+FLOPS = 2 * 2 * N * N * N
+
+F32 = mybir.dt.float32
+BF16 = mybir.dt.bfloat16
+U32 = mybir.dt.uint32
+U8 = mybir.dt.uint8
+FP8 = mybir.dt.float8_e4m3fn
+FP8X4 = mybir.dt.float8_e4m3fn_x4
+MULT = mybir.AluOpType.mult
+ADD = mybir.AluOpType.add
+COPY = mybir.ActivationFunctionType.Copy
+RELU = mybir.ActivationFunctionType.Relu
+
+P = 128
+TILES = N // P
+HALF = 512
+S_SHARE = 176
+
+
+def tile_gcniiinitialresidualidentitymap_kernel(tc, p, h, h0, g, w_bytes, w_scale, out):
+    nc = tc.nc
+    with ExitStack() as ctx:
+        keep = ctx.enter_context(tc.tile_pool(name="keep", bufs=1))
+        work = ctx.enter_context(tc.tile_pool(name="work", bufs=2))
+        outs = ctx.enter_context(tc.tile_pool(name="outs", bufs=4))
+        psum = ctx.enter_context(tc.psum_pool(name="psum", bufs=2))
+        ctx.enter_context(tc.manual_schedule())
+
+        def kept(name, shape, dtype):
+            return keep.tile(shape, dtype, name=name, tag=name, align_bytes=256)
+
+        ident = kept("ident", [P, P], F32)
+        g_bf = kept("g_bf", [P, 2, 4], BF16)
+        gain = kept("gain", [P, 2, 4], F32)
+        wsc = kept("wsc", [P, 2, 4], F32)
+        warm = kept("warm", [P, 8], F32)
+        p_raw = [kept("p_raw%d" % i, [P, N], BF16) for i in range(TILES)]
+        p_codes = [kept("p_codes%d" % i, [P, 2, P], U32) for i in range(TILES)]
+        p_scales = [kept("p_scales%d" % i, [P, 2, P], U8) for i in range(TILES)]
+        h0_raw = [kept("h0_raw%d" % i, [P, N], BF16) for i in range(TILES)]
+        q = [kept("q%d" % i, [P, N], F32) for i in range(TILES)]
+        pairs = [(a, b) for a in range(2) for b in range(2)]
+        h_raw = {ab: kept("h_raw%d%d" % ab, [P, 4, HALF], BF16) for ab in pairs}
+        h_grp = {ab: kept("h_grp%d%d" % ab, [P, HALF, 4], BF16) for ab in pairs}
+        h_codes = {ab: kept("h_codes%d%d" % ab, [P, HALF], U32) for ab in pairs}
+        h_scales = {ab: kept("h_scales%d%d" % ab, [P, HALF], U8) for ab in pairs}
+        w_raw = [kept("w_raw%d" % a, [P, 4, N], U8) for a in range(2)]
+        w_wide = {ab: kept("w_wide%d%d" % ab, [P, 4, HALF], BF16) for ab in pairs}
+        w_grp = {ab: kept("w_grp%d%d" % ab, [P, HALF, 4], BF16) for ab in pairs}
+        w_codes = {ab: kept("w_codes%d%d" % ab, [P, HALF], U32) for ab in pairs}
+        w_scales = {ab: kept("w_scales%d%d" % ab, [P, HALF], U8) for ab in pairs}
+        s_codes = {(i, a): kept("s_codes%d%d" % (i, a), [P, P], U32) for i in range(TILES) for a in range(2)}
+        s_scales = {(i, a): kept("s_scales%d%d" % (i, a), [P, P], U8) for i in range(TILES) for a in range(2)}
+
+        h_hbm = h.rearrange("(a p t) d -> a p t d", p=P, t=4)
+        w_hbm = w_bytes.rearrange("(a p t) e -> a p t e", p=P, t=4)
+
+        def load_p(i):
+            nc.sync.dma_start(out=p_raw[i][:], in_=p[i * P : (i + 1) * P, :])
+
+        def load_h0(i):
+            nc.sync.dma_start(out=h0_raw[i][:], in_=h0[i * P : (i + 1) * P, :])
+
+        def load_h(a, b):
+            nc.sync.dma_start(out=h_raw[a, b][:], in_=h_hbm[a][:, :, b * HALF : (b + 1) * HALF])
+
+        def load_w(a):
+            nc.sync.dma_start(out=w_raw[a][:], in_=w_hbm[a])
+
+        load_p(0)
+        load_h(0, 0)
+        load_h(1, 0)
+        load_p(1)
+        load_h0(0)
+        load_p(2)
+        load_h(0, 1)
+        load_p(3)
+        load_h0(1)
+        load_h(1, 1)
+        load_p(4)
+        load_h0(2)
+        load_p(5)
+        load_h0(3)
+        load_w(0)
+        load_p(6)
+        load_h0(4)
+        load_p(7)
+        load_h0(5)
+        load_w(1)
+        load_h0(6)
+        load_h0(7)
+        nc.scalar.dma_start(out=g_bf[:], in_=g.rearrange("(a p t) -> p a t", p=P, t=4))
+        nc.scalar.dma_start(out=wsc[:], in_=w_scale.rearrange("(a p t) o -> p a (t o)", p=P, t=4))
+
+        make_identity(nc, ident[:])
+        nc.gpsimd.tensor_scalar(out=gain[:], in0=g_bf[:], scalar1=0.3, scalar2=0.0, op0=MULT, op1=ADD)
+        nc.vector.memset(warm[:], 0.0)
+        nc.scalar.activation(out=warm[:], in_=warm[:], func=RELU, scale=1.0)
+
+        def s_interleave_h(a, b, lo, hi):
+            nc.scalar.copy(out=h_grp[a, b][:, lo:hi, :], in_=h_raw[a, b][:, :, lo:hi].rearrange("p t d -> p d t"))
+
+        def v_interleave_h(a, b, lo, hi):
+            nc.vector.tensor_copy(out=h_grp[a, b][:, lo:hi, :], in_=h_raw[a, b][:, :, lo:hi].rearrange("p t d -> p d t"))
+
+        def s_interleave_w(a, b, lo, hi):
+            nc.scalar.copy(out=w_grp[a, b][:, lo:hi, :], in_=w_wide[a, b][:, :, lo:hi].rearrange("p t d -> p d t"))
+
+        def v_interleave_w(a, b, lo, hi):
+            nc.vector.tensor_copy(out=w_grp[a, b][:, lo:hi, :], in_=w_wide[a, b][:, :, lo:hi].rearrange("p t d -> p d t"))
+
+        def widen_w(a, b, t):
+            nc.scalar.activation(
+                out=w_wide[a, b][:, t, :],
+                in_=w_raw[a][:, t, b * HALF : (b + 1) * HALF].bitcast(FP8),
+                func=COPY,
+                scale=wsc[:, a, t : t + 1],
+            )
+
+        def quantize(codes, scales, grouped):
+            nc.vector.quantize_mx(out=codes.bitcast(FP8X4), scales=scales, in_=grouped)
+
+        def quant_h(a, b):
+            quantize(h_codes[a, b][:], h_scales[a, b][:], h_grp[a, b][:].rearrange("p d t -> p (d t)"))
+
+        def quant_w(a, b):
+            quantize(w_codes[a, b][:], w_scales[a, b][:], w_grp[a, b][:].rearrange("p d t -> p (d t)"))
+
+        pt = {}
+        p_grp = {}
+        u = {}
+        tr = {}
+        s_grp = {}
+        tt = {}
+
+        def transpose_p(i):
+            pt[i] = psum.tile([P, 2, 2, P], F32, name="pt", tag="pt")
+            words = p_raw[i][:].bitcast(F32)
+            for a in range(2):
+                for half in range(2):
+                    nc.tensor.transpose(pt[i][:, a, half, :], words[:, 256 * a + half : 256 * (a + 1) : 2], ident[:])
+
+        def copy_p(i):
+            p_grp[i] = work.tile([P, 2, P, 4], BF16, name="p_grp", tag="p_grp", bufs=4, align_bytes=256)
+            nc.scalar.copy(
+                out=p_grp[i][:].rearrange("p a r t -> p (a r t)").bitcast(F32).rearrange("p (a r u) -> p a r u", a=2, u=2),
+                in_=pt[i][:].rearrange("p a u r -> p a r u"),
+            )
+
+        def quant_p(i):
+            quantize(
+                p_codes[i][:].rearrange("p a r -> p (a r)"),
+                p_scales[i][:].rearrange("p a r -> p (a r)"),
+                p_grp[i][:].rearrange("p a r t -> p (a r t)"),
+            )
+
+        def matmul1(m):
+            b, i = divmod(m, TILES)
+            u[m] = psum.tile([P, HALF], F32, name="u", tag="u")
+            for a in range(2):
+                nc.tensor.matmul_mx(
+                    out=u[m][:],
+                    lhsT=p_codes[i][:, a, :].bitcast(FP8X4),
+                    lhsT_scale=p_scales[i][:, a, :],
+                    rhs=h_codes[a, b][:].bitcast(FP8X4),
+                    rhs_scale=h_scales[a, b][:],
+                    start=(a == 0),
+                    stop=(a == 1),
+                )
+
+        def make_q(m):
+            b, i = divmod(m, TILES)
+            cols = slice(b * HALF, (b + 1) * HALF)
+            nc.vector.scalar_tensor_tensor(
+                out=q[i][:, cols], in0=u[m][:], scalar=7.0 / 3.0, in1=h0_raw[i][:, cols], op0=MULT, op1=ADD
+            )
+
+        def transpose_q(m):
+            b, i = divmod(m, TILES)
+            tr[m] = psum.tile([P, 4, P], F32, name="tr", tag="tr")
+            for t in range(4):
+                nc.tensor.transpose(tr[m][:, t, :], q[i][:, b * HALF + t : (b + 1) * HALF : 4], ident[:])
+
+        def make_sg(m):
+            b = m // TILES
+            s_grp[m] = work.tile([P, P, 4], BF16, name="s_grp", tag="s_grp", bufs=4, align_bytes=256)
+            nc.vector.tensor_tensor(
+                out=s_grp[m][:],
+                in0=tr[m][:].rearrange("p t r -> p r t"),
+                in1=gain[:, b, :].unsqueeze(1).to_broadcast([P, P, 4]),
+                op=MULT,
+            )
+
+        def quant_s(m):
+            b, i = divmod(m, TILES)
+            quantize(s_codes[i, b][:], s_scales[i, b][:], s_grp[m][:].rearrange("p r t -> p (r t)"))
+
+        def matmul2(i, b, tag):
+            tt[i, b] = psum.tile([P, HALF], F32, name="tt", tag=tag)
+            for a in range(2):
+                nc.tensor.matmul_mx(
+                    out=tt[i, b][:],
+                    lhsT=s_codes[i, a][:].bitcast(FP8X4),
+                    lhsT_scale=s_scales[i, a][:],
+                    rhs=w_codes[a, b][:].bitcast(FP8X4),
+                    rhs_scale=w_scales[a, b][:],
+                    start=(a == 0),
+                    stop=(a == 1),
+                )
+
+        def finish(i, b):
+            cols = slice(b * HALF, (b + 1) * HALF)
+            z = outs.tile([P, HALF], F32, name="z", tag="z")
+            nc.vector.scalar_tensor_tensor(
+                out=z[:], in0=tt[i, b][:], scalar=10.0 / 3.0, in1=q[i][:, cols], op0=MULT, op1=ADD
+            )
+            res = outs.tile([P, HALF], F32, name="res", tag="res")
+            nc.scalar.activation(out=res[:], in_=z[:], func=RELU, scale=0.15)
+            nc.sync.dma_start(out=out[i * P : (i + 1) * P, cols], in_=res[:])
+
+        transpose_p(0)
+        s_interleave_h(0, 0, 0, S_SHARE)
+        v_interleave_h(0, 0, S_SHARE, HALF)
+        copy_p(0)
+        s_interleave_h(1, 0, 0, S_SHARE)
+        quant_p(0)
+        quant_h(0, 0)
+        v_interleave_h(1, 0, S_SHARE, HALF)
+        transpose_p(1)
+        copy_p(1)
+        quant_p(1)
+        quant_h(1, 0)
+        matmul1(0)
+        transpose_p(2)
+        copy_p(2)
+
+        h_late = [(s_interleave_h, (a, 1, k * P, (k + 1) * P)) for a in range(2) for k in range(4)]
+        w_first = [(widen_w, (a, 0, t)) for a in range(2) for t in range(4)]
+        w_second = [(widen_w, (a, 1, t)) for a in range(2) for t in range(4)]
+        w_late = [(s_interleave_w, (a, 1, k * P, (k + 1) * P)) for a in range(2) for k in range(4)]
+        fill = {
+            0: h_late[0:2],
+            1: h_late[2:4],
+            2: h_late[4:6],
+            3: h_late[6:8] + [(quant_h, (0, 1))],
+            4: w_first[0:2],
+            5: w_first[2:4] + [(quant_h, (1, 1))],
+            6: w_first[4:6] + [(v_interleave_w, (0, 0, 0, HALF))],
+            7: w_first[6:8],
+            8: w_second[0:3] + [(quant_w, (0, 0))],
+            9: w_second[3:6] + [(v_interleave_w, (1, 0, 0, HALF))],
+            10: w_second[6:8] + w_late[0:1] + [(quant_w, (1, 0))],
+            11: w_late[1:3],
+            12: w_late[3:5],
+            13: w_late[5:7] + [(quant_w, (0, 1))],
+            14: w_late[7:8],
+            15: [(quant_w, (1, 1))],
+        }
+        last = 2 * TILES
+        for m in range(last + 3):
+            if m + 1 < last:
+                matmul1(m + 1)
+            if m < last:
+                make_q(m)
+                transpose_q(m)
+            if m + 3 < TILES:
+                transpose_p(m + 3)
+                copy_p(m + 3)
+            if m + 2 < TILES:
+                quant_p(m + 2)
+            if 0 <= m - 2 < last:
+                quant_s(m - 2)
+            if 0 <= m - 1 < last:
+                make_sg(m - 1)
+            for step, args in fill.get(m, []):
+                step(*args)
+            if TILES <= m - 2 < last:
+                matmul2(m - 2 - TILES, 0, "tt")
+            if TILES <= m - 3 < last:
+                finish(m - 3 - TILES, 0)
+        tags = ["u", "tr", "pt", "tt"]
+        for i in range(3):
+            matmul2(i, 1, tags[i % 4])
+        for i in range(TILES):
+            if i + 3 < TILES:
+                matmul2(i + 3, 1, tags[(i + 3) % 4])
+            finish(i, 1)

@@ -14,13 +14,25 @@ FP8 = mybir.dt.float8_e4m3fn
 FP8X4 = mybir.dt.float8_e4m3fn_x4
 MULT = mybir.AluOpType.mult
 ADD = mybir.AluOpType.add
+MAX = mybir.AluOpType.max
 COPY = mybir.ActivationFunctionType.Copy
 RELU = mybir.ActivationFunctionType.Relu
 
 P = 128
 TILES = N // P
 HALF = 512
-S_SHARE = 176
+S_SHARE = 240
+QUANT_H1 = (4, 5)
+QUANT_W = (15, 16, 18, 17)
+LATE_H = ((2, 'S'), (2, 'V'), (1, 'S'), (1, 'S'), (3, 'S'), (2, 'S'), (2, 'S'), (3, 'V'))
+WIDEN = (5, 3, 3, 4, 6, 5, 5, 7, 12, 5, 12, 12, 11, 11, 12, 11)
+MIX_W = ((7, 'S'), (8, 'S'), (7, 'V'), (6, 'V'), (7, 'S'), (10, 'S'), (15, 'S'), (11, 'V'), (13, 'S'), (12, 'S'), (15, 'S'), (16, 'S'), (12, 'S'), (12, 'S'), (13, 'S'), (14, 'S'))
+FORM = 'TTTTTTTTTTTTTTTT'
+COPY_P = 'SVSSSSSS'
+RELU_ON = 'SSSSSSSSSSSSSSSV'
+PT_LEAD = 4
+QS_LAG = 2
+MM2_STEP = (25, 37)
 
 
 def tile_gcniiinitialresidualidentitymap_kernel(tc, p, h, h0, g, w_bytes, w_scale, out):
@@ -28,16 +40,18 @@ def tile_gcniiinitialresidualidentitymap_kernel(tc, p, h, h0, g, w_bytes, w_scal
     with ExitStack() as ctx:
         keep = ctx.enter_context(tc.tile_pool(name="keep", bufs=1))
         work = ctx.enter_context(tc.tile_pool(name="work", bufs=2))
-        outs = ctx.enter_context(tc.tile_pool(name="outs", bufs=4))
+        outs = ctx.enter_context(tc.tile_pool(name="outs", bufs=8))
         psum = ctx.enter_context(tc.psum_pool(name="psum", bufs=2))
-        ctx.enter_context(tc.manual_schedule())
 
-        def kept(name, shape, dtype):
-            return keep.tile(shape, dtype, name=name, tag=name, align_bytes=256)
+        def kept(name, shape, dtype, tag=None):
+            return keep.tile(shape, dtype, name=name, tag=tag or name, align_bytes=256)
 
         ident = kept("ident", [P, P], F32)
         g_bf = kept("g_bf", [P, 2, 4], BF16)
         gain = kept("gain", [P, 2, 4], F32)
+        if "G" in FORM or "W" in FORM:
+            g_row = kept("g_row", [P, N], BF16)
+            gain_row = kept("gain_row", [P, N], F32)
         wsc = kept("wsc", [P, 2, 4], F32)
         warm = kept("warm", [P, 8], F32)
         p_raw = [kept("p_raw%d" % i, [P, N], BF16) for i in range(TILES)]
@@ -51,7 +65,7 @@ def tile_gcniiinitialresidualidentitymap_kernel(tc, p, h, h0, g, w_bytes, w_scal
         h_codes = {ab: kept("h_codes%d%d" % ab, [P, HALF], U32) for ab in pairs}
         h_scales = {ab: kept("h_scales%d%d" % ab, [P, HALF], U8) for ab in pairs}
         w_raw = [kept("w_raw%d" % a, [P, 4, N], U8) for a in range(2)]
-        w_wide = {ab: kept("w_wide%d%d" % ab, [P, 4, HALF], BF16) for ab in pairs}
+        w_wide = {}
         w_grp = {ab: kept("w_grp%d%d" % ab, [P, HALF, 4], BF16) for ab in pairs}
         w_codes = {ab: kept("w_codes%d%d" % ab, [P, HALF], U32) for ab in pairs}
         w_scales = {ab: kept("w_scales%d%d" % ab, [P, HALF], U8) for ab in pairs}
@@ -73,49 +87,51 @@ def tile_gcniiinitialresidualidentitymap_kernel(tc, p, h, h0, g, w_bytes, w_scal
         def load_w(a):
             nc.sync.dma_start(out=w_raw[a][:], in_=w_hbm[a])
 
+        load_p(1)
         load_p(0)
         load_h(0, 0)
+        load_h0(1)
         load_h(1, 0)
-        load_p(1)
         load_h0(0)
         load_p(2)
-        load_h(0, 1)
         load_p(3)
-        load_h0(1)
-        load_h(1, 1)
-        load_p(4)
-        load_h0(2)
         load_p(5)
-        load_h0(3)
-        load_w(0)
+        load_h0(2)
+        load_p(4)
         load_p(6)
+        nc.sync.dma_start(out=g_bf[:], in_=g.rearrange("(a p t) -> p a t", p=P, t=4))
+        nc.sync.dma_start(out=wsc[:], in_=w_scale.rearrange("(a p t) o -> p a (t o)", p=P, t=4))
+        load_h(0, 1)
+        load_h0(3)
+        load_h(1, 1)
         load_h0(4)
         load_p(7)
         load_h0(5)
-        load_w(1)
+        load_w(0)
         load_h0(6)
+        load_w(1)
         load_h0(7)
-        nc.scalar.dma_start(out=g_bf[:], in_=g.rearrange("(a p t) -> p a t", p=P, t=4))
-        nc.scalar.dma_start(out=wsc[:], in_=w_scale.rearrange("(a p t) o -> p a (t o)", p=P, t=4))
 
         make_identity(nc, ident[:])
         nc.gpsimd.tensor_scalar(out=gain[:], in0=g_bf[:], scalar1=0.3, scalar2=0.0, op0=MULT, op1=ADD)
+        if "G" in FORM or "W" in FORM:
+            nc.gpsimd.tensor_scalar(out=gain_row[:], in0=g_row[:], scalar1=0.3, scalar2=0.0, op0=MULT, op1=ADD)
         nc.vector.memset(warm[:], 0.0)
         nc.scalar.activation(out=warm[:], in_=warm[:], func=RELU, scale=1.0)
 
-        def s_interleave_h(a, b, lo, hi):
-            nc.scalar.copy(out=h_grp[a, b][:, lo:hi, :], in_=h_raw[a, b][:, :, lo:hi].rearrange("p t d -> p d t"))
-
-        def v_interleave_h(a, b, lo, hi):
-            nc.vector.tensor_copy(out=h_grp[a, b][:, lo:hi, :], in_=h_raw[a, b][:, :, lo:hi].rearrange("p t d -> p d t"))
-
-        def s_interleave_w(a, b, lo, hi):
-            nc.scalar.copy(out=w_grp[a, b][:, lo:hi, :], in_=w_wide[a, b][:, :, lo:hi].rearrange("p t d -> p d t"))
-
-        def v_interleave_w(a, b, lo, hi):
-            nc.vector.tensor_copy(out=w_grp[a, b][:, lo:hi, :], in_=w_wide[a, b][:, :, lo:hi].rearrange("p t d -> p d t"))
+        def interleave(engine, grouped, raw, lo, hi):
+            dst = grouped[:, lo:hi, :].rearrange("p (c i) t -> p c t i", i=4)
+            src = raw[:, :, lo:hi].rearrange("p t (c i) -> p c t i", i=4)
+            if engine == "V":
+                nc.vector.tensor_copy(out=dst, in_=src)
+            elif engine == "S":
+                nc.scalar.copy(out=dst, in_=src)
+            else:
+                nc.gpsimd.tensor_scalar(out=dst, in0=src, scalar1=1.0, scalar2=0.0, op0=MULT, op1=ADD)
 
         def widen_w(a, b, t):
+            if (a, b) not in w_wide:
+                w_wide[a, b] = kept("w_wide%d%d" % (a, b), [P, 4, HALF], BF16, tag="h_raw%d%d" % (a, b))
             nc.scalar.activation(
                 out=w_wide[a, b][:, t, :],
                 in_=w_raw[a][:, t, b * HALF : (b + 1) * HALF].bitcast(FP8),
@@ -148,10 +164,12 @@ def tile_gcniiinitialresidualidentitymap_kernel(tc, p, h, h0, g, w_bytes, w_scal
 
         def copy_p(i):
             p_grp[i] = work.tile([P, 2, P, 4], BF16, name="p_grp", tag="p_grp", bufs=4, align_bytes=256)
-            nc.scalar.copy(
-                out=p_grp[i][:].rearrange("p a r t -> p (a r t)").bitcast(F32).rearrange("p (a r u) -> p a r u", a=2, u=2),
-                in_=pt[i][:].rearrange("p a u r -> p a r u"),
-            )
+            dst = p_grp[i][:].rearrange("p a r t -> p (a r t)").bitcast(F32).rearrange("p (a r u) -> p a r u", a=2, u=2)
+            src = pt[i][:].rearrange("p a u r -> p a r u")
+            if COPY_P[i] == "V":
+                nc.vector.tensor_copy(out=dst, in_=src)
+            else:
+                nc.scalar.copy(out=dst, in_=src)
 
         def quant_p(i):
             quantize(
@@ -197,6 +215,28 @@ def tile_gcniiinitialresidualidentitymap_kernel(tc, p, h, h0, g, w_bytes, w_scal
                 op=MULT,
             )
 
+        sg = {}
+
+        def make_sg_row(m):
+            b, i = divmod(m, TILES)
+            cols = slice(b * HALF, (b + 1) * HALF)
+            sg[m] = work.tile([P, HALF], BF16, name="sg", tag="sg", bufs=3, align_bytes=256)
+            engine = nc.gpsimd if FORM[m] == "G" else nc.vector
+            engine.tensor_tensor(out=sg[m][:], in0=q[i][:, cols], in1=gain_row[:, cols], op=MULT)
+
+        def transpose_sg(m):
+            tr[m] = psum.tile([P, 2, P], F32, name="tr", tag="tr")
+            words = sg[m][:].bitcast(F32)
+            for half in range(2):
+                nc.tensor.transpose(tr[m][:, half, :], words[:, half::2], ident[:])
+
+        def copy_sg(m):
+            s_grp[m] = work.tile([P, P, 4], BF16, name="s_grp", tag="s_grp", bufs=4, align_bytes=256)
+            nc.scalar.copy(
+                out=s_grp[m][:].rearrange("p r t -> p (r t)").bitcast(F32).rearrange("p (r u) -> p r u", u=2),
+                in_=tr[m][:].rearrange("p u r -> p r u"),
+            )
+
         def quant_s(m):
             b, i = divmod(m, TILES)
             quantize(s_codes[i, b][:], s_scales[i, b][:], s_grp[m][:].rearrange("p r t -> p (r t)"))
@@ -221,73 +261,88 @@ def tile_gcniiinitialresidualidentitymap_kernel(tc, p, h, h0, g, w_bytes, w_scal
                 out=z[:], in0=tt[i, b][:], scalar=10.0 / 3.0, in1=q[i][:, cols], op0=MULT, op1=ADD
             )
             res = outs.tile([P, HALF], F32, name="res", tag="res")
-            nc.scalar.activation(out=res[:], in_=z[:], func=RELU, scale=0.15)
+            if RELU_ON[b * TILES + i] == "G":
+                nc.gpsimd.tensor_scalar(out=res[:], in0=z[:], scalar1=0.15, scalar2=0.0, op0=MULT, op1=MAX)
+            elif RELU_ON[b * TILES + i] == "V":
+                nc.vector.tensor_scalar(out=res[:], in0=z[:], scalar1=0.15, scalar2=0.0, op0=MULT, op1=MAX)
+            else:
+                nc.scalar.activation(out=res[:], in_=z[:], func=RELU, scale=0.15)
             nc.sync.dma_start(out=out[i * P : (i + 1) * P, cols], in_=res[:])
 
-        transpose_p(0)
-        s_interleave_h(0, 0, 0, S_SHARE)
-        v_interleave_h(0, 0, S_SHARE, HALF)
-        copy_p(0)
-        s_interleave_h(1, 0, 0, S_SHARE)
-        quant_p(0)
-        quant_h(0, 0)
-        v_interleave_h(1, 0, S_SHARE, HALF)
-        transpose_p(1)
-        copy_p(1)
-        quant_p(1)
-        quant_h(1, 0)
-        matmul1(0)
-        transpose_p(2)
-        copy_p(2)
+        def fill(m):
+            for k, step in enumerate(QUANT_H1):
+                if step == m:
+                    quant_h(k, 1)
+            for k, step in enumerate(QUANT_W):
+                if step == m:
+                    quant_w(k % 2, k // 2)
+            for k, (step, engine) in enumerate(LATE_H):
+                if step == m:
+                    ab = (k // 4, 1)
+                    interleave(engine, h_grp[ab], h_raw[ab], (k % 4) * P, (k % 4 + 1) * P)
+            for k, step in enumerate(WIDEN):
+                if step == m:
+                    widen_w((k % 8) // 4, k // 8, k % 4)
+            for k, (step, engine) in enumerate(MIX_W):
+                if step == m:
+                    ab = ((k % 8) // 4, k // 8)
+                    interleave(engine, w_grp[ab], w_wide[ab], (k % 4) * P, (k % 4 + 1) * P)
 
-        h_late = [(s_interleave_h, (a, 1, k * P, (k + 1) * P)) for a in range(2) for k in range(4)]
-        w_first = [(widen_w, (a, 0, t)) for a in range(2) for t in range(4)]
-        w_second = [(widen_w, (a, 1, t)) for a in range(2) for t in range(4)]
-        w_late = [(s_interleave_w, (a, 1, k * P, (k + 1) * P)) for a in range(2) for k in range(4)]
-        fill = {
-            0: h_late[0:2],
-            1: h_late[2:4],
-            2: h_late[4:6],
-            3: h_late[6:8] + [(quant_h, (0, 1))],
-            4: w_first[0:2],
-            5: w_first[2:4] + [(quant_h, (1, 1))],
-            6: w_first[4:6] + [(v_interleave_w, (0, 0, 0, HALF))],
-            7: w_first[6:8],
-            8: w_second[0:3] + [(quant_w, (0, 0))],
-            9: w_second[3:6] + [(v_interleave_w, (1, 0, 0, HALF))],
-            10: w_second[6:8] + w_late[0:1] + [(quant_w, (1, 0))],
-            11: w_late[1:3],
-            12: w_late[3:5],
-            13: w_late[5:7] + [(quant_w, (0, 1))],
-            14: w_late[7:8],
-            15: [(quant_w, (1, 1))],
-        }
         last = 2 * TILES
-        for m in range(last + 3):
-            if m + 1 < last:
+        for m in range(-PT_LEAD, last + 10):
+            if 0 <= m + 1 < last:
                 matmul1(m + 1)
-            if m < last:
+            if 0 <= m < last:
                 make_q(m)
-                transpose_q(m)
-            if m + 3 < TILES:
-                transpose_p(m + 3)
-                copy_p(m + 3)
-            if m + 2 < TILES:
+                if FORM[m] == "T":
+                    transpose_q(m)
+                elif FORM[m] == "G":
+                    make_sg_row(m)
+            if 0 <= m - 1 < last and FORM[m - 1] == "G":
+                transpose_sg(m - 1)
+                copy_sg(m - 1)
+            if 0 <= m + PT_LEAD < TILES:
+                transpose_p(m + PT_LEAD)
+                copy_p(m + PT_LEAD)
+            if 0 <= m + 2 < TILES:
                 quant_p(m + 2)
-            if 0 <= m - 2 < last:
-                quant_s(m - 2)
+            if m == -4:
+                interleave("S", h_grp[0, 0], h_raw[0, 0], 0, S_SHARE)
+                interleave("V", h_grp[0, 0], h_raw[0, 0], S_SHARE, HALF)
+            if m == -3:
+                quant_h(0, 0)
+                interleave("S", h_grp[1, 0], h_raw[1, 0], 0, S_SHARE)
+                interleave("V", h_grp[1, 0], h_raw[1, 0], S_SHARE, HALF)
+            if m == -2:
+                quant_h(1, 0)
+            if 0 <= m - QS_LAG < last:
+                quant_s(m - QS_LAG)
             if 0 <= m - 1 < last:
-                make_sg(m - 1)
-            for step, args in fill.get(m, []):
-                step(*args)
-            if TILES <= m - 2 < last:
-                matmul2(m - 2 - TILES, 0, "tt")
-            if TILES <= m - 3 < last:
-                finish(m - 3 - TILES, 0)
+                if FORM[m - 1] == "T":
+                    make_sg(m - 1)
+                elif FORM[m - 1] == "W":
+                    make_sg_row(m - 1)
+            if 0 <= m - 1 < last and FORM[m - 1] == "W":
+                transpose_sg(m - 1)
+                copy_sg(m - 1)
+            fill(m)
+            for b in range(2):
+                i = m - MM2_STEP[b]
+                if 0 <= i < TILES and m <= last + 2:
+                    matmul2(i, b, "pt" if b else "tt")
+                i = m - MM2_STEP[b] - 1
+                if 0 <= i < TILES and m <= last + 2:
+                    finish(i, b)
+            if m == last + 2:
+                break
+        rest = [(i, b) for b in range(2) for i in range(TILES) if i + MM2_STEP[b] + 1 > last + 2]
+        pend = [x for x in rest if x[0] + MM2_STEP[x[1]] > last + 2]
         tags = ["u", "tr", "pt", "tt"]
-        for i in range(3):
-            matmul2(i, 1, tags[i % 4])
-        for i in range(TILES):
-            if i + 3 < TILES:
-                matmul2(i + 3, 1, tags[(i + 3) % 4])
-            finish(i, 1)
+        for k in range(min(3, len(pend))):
+            matmul2(pend[k][0], pend[k][1], tags[k % 4])
+        nxt = 3
+        for k, (i, b) in enumerate(rest):
+            finish(i, b)
+            if nxt < len(pend):
+                matmul2(pend[nxt][0], pend[nxt][1], tags[nxt % 4])
+                nxt += 1

@@ -21,18 +21,24 @@ RELU = mybir.ActivationFunctionType.Relu
 P = 128
 TILES = N // P
 HALF = 512
-S_SHARE = 240
-QUANT_H1 = (4, 5)
-QUANT_W = (15, 16, 18, 17)
-LATE_H = ((2, 'S'), (2, 'V'), (1, 'S'), (1, 'S'), (3, 'S'), (2, 'S'), (2, 'S'), (3, 'V'))
-WIDEN = (5, 3, 3, 4, 6, 5, 5, 7, 12, 5, 12, 12, 11, 11, 12, 11)
-MIX_W = ((7, 'S'), (8, 'S'), (7, 'V'), (6, 'V'), (7, 'S'), (10, 'S'), (15, 'S'), (11, 'V'), (13, 'S'), (12, 'S'), (15, 'S'), (16, 'S'), (12, 'S'), (12, 'S'), (13, 'S'), (14, 'S'))
+P_GROUPS = ((0, 1), (1, 2), (2, 4), (4, 6), (6, 8))
+H0_GROUPS = ((0, 2), (2, 4), (4, 6), (6, 8))
+H_FULL = 'FF'
+BYTES_OF = {'p0': 500, 'p1': 500, 'p2': 933, 'p3': 933, 'p4': 933, 'r0': 933, 'r1': 933, 'r2': 933, 'r3': 933, 'h0': 1790, 'h1': 1790, 'w0': 933, 'w1': 933, 'S': 800, 'GR': 500}
+W = {'hi': {'V': 281, 'S': 515}, 'wi': {'V': 281, 'S': 515}, 'wd': {'S': 447}, 'qh': {'V': 463}, 'qw': {'V': 463}, 'pt': {'T': 424}, 'cp': {'V': 442, 'S': 447}, 'qp': {'V': 237}, 'm1': {'T': 440}, 'q': {'V': 442}, 'gg': {'G': 915}, 'ts': {'T': 212}, 'cs': {'S': 235}, 'tr': {'T': 424}, 'sg': {'V': 442}, 'qs': {'V': 237}, 'm2': {'T': 440}, 'z': {'V': 442}, 're': {'S': 447}}
+LOADS = ('h10', 'h00', 'p0', 'p2', 'p1', 'w1', 'r0', 'S', 'r1', 'r2', 'p3', 'p4', 'w0', 'r3')
 FORM = 'TTTTTTTTTTTTTTTT'
-COPY_P = 'SVSSSSSS'
-RELU_ON = 'SSSSSSSSSSSSSSSV'
-PT_LEAD = 4
-QS_LAG = 2
-MM2_STEP = (25, 37)
+FAMILIES = ("hi", "wi", "wd", "qh", "qw", "pt", "cp", "qp", "gg", "ts", "cs", "tr", "sg", "qs", "re", "m", "q", "z")
+BIAS = {'z': -500, 'gg': 18500, 'tr': 500, 'hi': 0, 'cs': -1500, 're': 6000, 'wi': -4500, 'qh': 3500, 'sg': 500, 'qp': -4000, 'q': 7500, 'qs': 9000, 'ts': -12500, 'cp': 4500, 'pt': -15500, 'm': 11000, 'qw': 7000, 'wd': -1000}
+TILE_BIAS = 1000
+FLEX = 10000
+KEEP = 2000
+WAIT = 180
+SWITCH = 95
+HEAD = 1500
+NEVER = 1000000000
+WINDOW = {'V': 0, 'S': 50, 'T': 0, 'G': 0}
+OUT_BUFS = 8
 
 
 def tile_gcniiinitialresidualidentitymap_kernel(tc, p, h, h0, g, w_bytes, w_scale, out):
@@ -40,8 +46,9 @@ def tile_gcniiinitialresidualidentitymap_kernel(tc, p, h, h0, g, w_bytes, w_scal
     with ExitStack() as ctx:
         keep = ctx.enter_context(tc.tile_pool(name="keep", bufs=1))
         work = ctx.enter_context(tc.tile_pool(name="work", bufs=2))
-        outs = ctx.enter_context(tc.tile_pool(name="outs", bufs=8))
-        psum = ctx.enter_context(tc.psum_pool(name="psum", bufs=2))
+        outs = ctx.enter_context(tc.tile_pool(name="outs", bufs=OUT_BUFS))
+        psum = ctx.enter_context(tc.psum_pool(name="psum", bufs=1))
+        ctx.enter_context(tc.manual_schedule())
 
         def kept(name, shape, dtype, tag=None):
             return keep.tile(shape, dtype, name=name, tag=tag or name, align_bytes=256)
@@ -49,18 +56,32 @@ def tile_gcniiinitialresidualidentitymap_kernel(tc, p, h, h0, g, w_bytes, w_scal
         ident = kept("ident", [P, P], F32)
         g_bf = kept("g_bf", [P, 2, 4], BF16)
         gain = kept("gain", [P, 2, 4], F32)
-        if "G" in FORM or "W" in FORM:
+        if "G" in FORM:
             g_row = kept("g_row", [P, N], BF16)
             gain_row = kept("gain_row", [P, N], F32)
         wsc = kept("wsc", [P, 2, 4], F32)
         warm = kept("warm", [P, 8], F32)
-        p_raw = [kept("p_raw%d" % i, [P, N], BF16) for i in range(TILES)]
+        p_raw, p_tile = {}, {}
+        h0_raw, h0_tile = {}, {}
+        for name, groups, rows, tiles in (("p_raw", P_GROUPS, p_raw, p_tile), ("h0_raw", H0_GROUPS, h0_raw, h0_tile)):
+            for lo, hi in groups:
+                tiles[lo] = kept("%s%d" % (name, lo), [P, hi - lo, N], BF16)
+                for i in range(lo, hi):
+                    rows[i] = tiles[lo][:, i - lo, :]
         p_codes = [kept("p_codes%d" % i, [P, 2, P], U32) for i in range(TILES)]
         p_scales = [kept("p_scales%d" % i, [P, 2, P], U8) for i in range(TILES)]
-        h0_raw = [kept("h0_raw%d" % i, [P, N], BF16) for i in range(TILES)]
         q = [kept("q%d" % i, [P, N], F32) for i in range(TILES)]
         pairs = [(a, b) for a in range(2) for b in range(2)]
-        h_raw = {ab: kept("h_raw%d%d" % ab, [P, 4, HALF], BF16) for ab in pairs}
+        h_raw = {}
+        h_whole = {}
+        for a in range(2):
+            if H_FULL[a] == "F":
+                h_whole[a] = kept("h_raw%d" % a, [P, 4, N], BF16)
+                for b in range(2):
+                    h_raw[a, b] = h_whole[a][:, :, b * HALF : (b + 1) * HALF]
+            else:
+                for b in range(2):
+                    h_raw[a, b] = kept("h_raw%d%d" % (a, b), [P, 4, HALF], BF16)[:]
         h_grp = {ab: kept("h_grp%d%d" % ab, [P, HALF, 4], BF16) for ab in pairs}
         h_codes = {ab: kept("h_codes%d%d" % ab, [P, HALF], U32) for ab in pairs}
         h_scales = {ab: kept("h_scales%d%d" % ab, [P, HALF], U8) for ab in pairs}
@@ -69,59 +90,60 @@ def tile_gcniiinitialresidualidentitymap_kernel(tc, p, h, h0, g, w_bytes, w_scal
         w_grp = {ab: kept("w_grp%d%d" % ab, [P, HALF, 4], BF16) for ab in pairs}
         w_codes = {ab: kept("w_codes%d%d" % ab, [P, HALF], U32) for ab in pairs}
         w_scales = {ab: kept("w_scales%d%d" % ab, [P, HALF], U8) for ab in pairs}
-        s_codes = {(i, a): kept("s_codes%d%d" % (i, a), [P, P], U32) for i in range(TILES) for a in range(2)}
-        s_scales = {(i, a): kept("s_scales%d%d" % (i, a), [P, P], U8) for i in range(TILES) for a in range(2)}
+        s_codes = [kept("s_codes%d" % i, [P, 2, P], U32) for i in range(TILES)]
+        s_scales = [kept("s_scales%d" % i, [P, 2, P], U8) for i in range(TILES)]
 
         h_hbm = h.rearrange("(a p t) d -> a p t d", p=P, t=4)
         w_hbm = w_bytes.rearrange("(a p t) e -> a p t e", p=P, t=4)
 
-        def load_p(i):
-            nc.sync.dma_start(out=p_raw[i][:], in_=p[i * P : (i + 1) * P, :])
+        p_hbm = p.rearrange("(r i) k -> r i k", i=TILES)
+        h0_hbm = h0.rearrange("(r i) d -> r i d", i=TILES)
+        out_hbm = out.rearrange("(r i) e -> r i e", i=TILES)
 
-        def load_h0(i):
-            nc.sync.dma_start(out=h0_raw[i][:], in_=h0[i * P : (i + 1) * P, :])
+        def load_p(k):
+            lo, hi = P_GROUPS[k]
+            nc.sync.dma_start(out=p_tile[lo][:], in_=p_hbm[:, lo:hi, :])
+
+        def load_h0(k):
+            lo, hi = H0_GROUPS[k]
+            nc.sync.dma_start(out=h0_tile[lo][:], in_=h0_hbm[:, lo:hi, :])
 
         def load_h(a, b):
-            nc.sync.dma_start(out=h_raw[a, b][:], in_=h_hbm[a][:, :, b * HALF : (b + 1) * HALF])
+            if H_FULL[a] == "F":
+                if b == 0:
+                    nc.sync.dma_start(out=h_whole[a][:], in_=h_hbm[a])
+            else:
+                nc.sync.dma_start(out=h_raw[a, b], in_=h_hbm[a][:, :, b * HALF : (b + 1) * HALF])
 
         def load_w(a):
             nc.sync.dma_start(out=w_raw[a][:], in_=w_hbm[a])
 
-        load_p(1)
-        load_p(0)
-        load_h(0, 0)
-        load_h0(1)
         load_h(1, 0)
-        load_h0(0)
+        load_h(0, 0)
+        load_p(0)
         load_p(2)
-        load_p(3)
-        load_p(5)
-        load_h0(2)
-        load_p(4)
-        load_p(6)
+        load_p(1)
+        load_w(1)
+        load_h0(0)
         nc.sync.dma_start(out=g_bf[:], in_=g.rearrange("(a p t) -> p a t", p=P, t=4))
         nc.sync.dma_start(out=wsc[:], in_=w_scale.rearrange("(a p t) o -> p a (t o)", p=P, t=4))
-        load_h(0, 1)
-        load_h0(3)
-        load_h(1, 1)
-        load_h0(4)
-        load_p(7)
-        load_h0(5)
+        load_h0(1)
+        load_h0(2)
+        load_p(3)
+        load_p(4)
         load_w(0)
-        load_h0(6)
-        load_w(1)
-        load_h0(7)
+        load_h0(3)
 
         make_identity(nc, ident[:])
         nc.gpsimd.tensor_scalar(out=gain[:], in0=g_bf[:], scalar1=0.3, scalar2=0.0, op0=MULT, op1=ADD)
-        if "G" in FORM or "W" in FORM:
+        if "G" in FORM:
             nc.gpsimd.tensor_scalar(out=gain_row[:], in0=g_row[:], scalar1=0.3, scalar2=0.0, op0=MULT, op1=ADD)
         nc.vector.memset(warm[:], 0.0)
         nc.scalar.activation(out=warm[:], in_=warm[:], func=RELU, scale=1.0)
 
         def interleave(engine, grouped, raw, lo, hi):
-            dst = grouped[:, lo:hi, :].rearrange("p (c i) t -> p c t i", i=4)
-            src = raw[:, :, lo:hi].rearrange("p t (c i) -> p c t i", i=4)
+            dst = grouped[:, lo:hi, :]
+            src = raw[:, :, lo:hi].rearrange("p t d -> p d t")
             if engine == "V":
                 nc.vector.tensor_copy(out=dst, in_=src)
             elif engine == "S":
@@ -131,7 +153,7 @@ def tile_gcniiinitialresidualidentitymap_kernel(tc, p, h, h0, g, w_bytes, w_scal
 
         def widen_w(a, b, t):
             if (a, b) not in w_wide:
-                w_wide[a, b] = kept("w_wide%d%d" % (a, b), [P, 4, HALF], BF16, tag="h_raw%d%d" % (a, b))
+                w_wide[a, b] = kept("w_wide%d%d" % (a, b), [P, 4, HALF], BF16, tag=None if "F" in H_FULL else "h_raw%d%d" % (a, b))
             nc.scalar.activation(
                 out=w_wide[a, b][:, t, :],
                 in_=w_raw[a][:, t, b * HALF : (b + 1) * HALF].bitcast(FP8),
@@ -155,18 +177,18 @@ def tile_gcniiinitialresidualidentitymap_kernel(tc, p, h, h0, g, w_bytes, w_scal
         s_grp = {}
         tt = {}
 
-        def transpose_p(i):
-            pt[i] = psum.tile([P, 2, 2, P], F32, name="pt", tag="pt")
-            words = p_raw[i][:].bitcast(F32)
+        def transpose_p(i, bank):
+            pt[i] = psum.tile([P, 2, 2, P], F32, name="pt", tag="bank%d" % bank)
+            words = p_raw[i].bitcast(F32)
             for a in range(2):
                 for half in range(2):
                     nc.tensor.transpose(pt[i][:, a, half, :], words[:, 256 * a + half : 256 * (a + 1) : 2], ident[:])
 
-        def copy_p(i):
+        def copy_p(i, engine):
             p_grp[i] = work.tile([P, 2, P, 4], BF16, name="p_grp", tag="p_grp", bufs=4, align_bytes=256)
             dst = p_grp[i][:].rearrange("p a r t -> p (a r t)").bitcast(F32).rearrange("p (a r u) -> p a r u", a=2, u=2)
             src = pt[i][:].rearrange("p a u r -> p a r u")
-            if COPY_P[i] == "V":
+            if engine == "V":
                 nc.vector.tensor_copy(out=dst, in_=src)
             else:
                 nc.scalar.copy(out=dst, in_=src)
@@ -178,9 +200,9 @@ def tile_gcniiinitialresidualidentitymap_kernel(tc, p, h, h0, g, w_bytes, w_scal
                 p_grp[i][:].rearrange("p a r t -> p (a r t)"),
             )
 
-        def matmul1(m):
-            b, i = divmod(m, TILES)
-            u[m] = psum.tile([P, HALF], F32, name="u", tag="u")
+        def matmul1(m, bank):
+            i, b = divmod(m, 2)
+            u[m] = psum.tile([P, HALF], F32, name="u", tag="bank%d" % bank)
             for a in range(2):
                 nc.tensor.matmul_mx(
                     out=u[m][:],
@@ -193,156 +215,229 @@ def tile_gcniiinitialresidualidentitymap_kernel(tc, p, h, h0, g, w_bytes, w_scal
                 )
 
         def make_q(m):
-            b, i = divmod(m, TILES)
+            i, b = divmod(m, 2)
             cols = slice(b * HALF, (b + 1) * HALF)
             nc.vector.scalar_tensor_tensor(
                 out=q[i][:, cols], in0=u[m][:], scalar=7.0 / 3.0, in1=h0_raw[i][:, cols], op0=MULT, op1=ADD
             )
 
-        def transpose_q(m):
-            b, i = divmod(m, TILES)
-            tr[m] = psum.tile([P, 4, P], F32, name="tr", tag="tr")
+        def transpose_q(m, bank):
+            i, b = divmod(m, 2)
+            tr[m] = psum.tile([P, 4, P], F32, name="tr", tag="bank%d" % bank)
             for t in range(4):
                 nc.tensor.transpose(tr[m][:, t, :], q[i][:, b * HALF + t : (b + 1) * HALF : 4], ident[:])
 
-        def make_sg(m):
-            b = m // TILES
-            s_grp[m] = work.tile([P, P, 4], BF16, name="s_grp", tag="s_grp", bufs=4, align_bytes=256)
-            nc.vector.tensor_tensor(
-                out=s_grp[m][:],
-                in0=tr[m][:].rearrange("p t r -> p r t"),
-                in1=gain[:, b, :].unsqueeze(1).to_broadcast([P, P, 4]),
-                op=MULT,
-            )
-
         sg = {}
 
-        def make_sg_row(m):
-            b, i = divmod(m, TILES)
+        def s_group(i):
+            if i not in s_grp:
+                s_grp[i] = work.tile([P, 2, P, 4], BF16, name="s_grp", tag="s_grp", bufs=4, align_bytes=256)
+            return s_grp[i]
+
+        def gain_on_gpsimd(m):
+            i, b = divmod(m, 2)
             cols = slice(b * HALF, (b + 1) * HALF)
             sg[m] = work.tile([P, HALF], BF16, name="sg", tag="sg", bufs=3, align_bytes=256)
-            engine = nc.gpsimd if FORM[m] == "G" else nc.vector
-            engine.tensor_tensor(out=sg[m][:], in0=q[i][:, cols], in1=gain_row[:, cols], op=MULT)
+            nc.gpsimd.tensor_tensor(out=sg[m][:], in0=q[i][:, cols], in1=gain_row[:, cols], op=MULT)
 
-        def transpose_sg(m):
-            tr[m] = psum.tile([P, 2, P], F32, name="tr", tag="tr")
+        def transpose_sg(m, bank):
+            tr[m] = psum.tile([P, 2, P], F32, name="tr", tag="bank%d" % bank)
             words = sg[m][:].bitcast(F32)
             for half in range(2):
                 nc.tensor.transpose(tr[m][:, half, :], words[:, half::2], ident[:])
 
         def copy_sg(m):
-            s_grp[m] = work.tile([P, P, 4], BF16, name="s_grp", tag="s_grp", bufs=4, align_bytes=256)
+            i, b = divmod(m, 2)
             nc.scalar.copy(
-                out=s_grp[m][:].rearrange("p r t -> p (r t)").bitcast(F32).rearrange("p (r u) -> p r u", u=2),
+                out=s_group(i)[:, b].rearrange("p r t -> p (r t)").bitcast(F32).rearrange("p (r u) -> p r u", u=2),
                 in_=tr[m][:].rearrange("p u r -> p r u"),
             )
 
-        def quant_s(m):
-            b, i = divmod(m, TILES)
-            quantize(s_codes[i, b][:], s_scales[i, b][:], s_grp[m][:].rearrange("p r t -> p (r t)"))
+        def make_sg(m):
+            i, b = divmod(m, 2)
+            s_group(i)
+            nc.vector.tensor_tensor(
+                out=s_grp[i][:, b],
+                in0=tr[m][:].rearrange("p t r -> p r t"),
+                in1=gain[:, b, :].unsqueeze(1).to_broadcast([P, P, 4]),
+                op=MULT,
+            )
 
-        def matmul2(i, b, tag):
-            tt[i, b] = psum.tile([P, HALF], F32, name="tt", tag=tag)
+        def quant_s(i):
+            quantize(
+                s_codes[i][:].rearrange("p a r -> p (a r)"),
+                s_scales[i][:].rearrange("p a r -> p (a r)"),
+                s_grp[i][:].rearrange("p a r t -> p (a r t)"),
+            )
+
+        def matmul2(i, b, bank):
+            tt[i, b] = psum.tile([P, HALF], F32, name="tt", tag="bank%d" % bank)
             for a in range(2):
                 nc.tensor.matmul_mx(
                     out=tt[i, b][:],
-                    lhsT=s_codes[i, a][:].bitcast(FP8X4),
-                    lhsT_scale=s_scales[i, a][:],
+                    lhsT=s_codes[i][:, a, :].bitcast(FP8X4),
+                    lhsT_scale=s_scales[i][:, a, :],
                     rhs=w_codes[a, b][:].bitcast(FP8X4),
                     rhs_scale=w_scales[a, b][:],
                     start=(a == 0),
                     stop=(a == 1),
                 )
 
-        def finish(i, b):
-            cols = slice(b * HALF, (b + 1) * HALF)
-            z = outs.tile([P, HALF], F32, name="z", tag="z")
+        rows = {}
+
+        def make_z(i, b):
+            rows[i, b] = outs.tile([P, HALF], F32, name="row", tag="row")
             nc.vector.scalar_tensor_tensor(
-                out=z[:], in0=tt[i, b][:], scalar=10.0 / 3.0, in1=q[i][:, cols], op0=MULT, op1=ADD
+                out=rows[i, b][:],
+                in0=tt[i, b][:],
+                scalar=10.0 / 3.0,
+                in1=q[i][:, b * HALF : (b + 1) * HALF],
+                op0=MULT,
+                op1=ADD,
             )
-            res = outs.tile([P, HALF], F32, name="res", tag="res")
-            if RELU_ON[b * TILES + i] == "G":
-                nc.gpsimd.tensor_scalar(out=res[:], in0=z[:], scalar1=0.15, scalar2=0.0, op0=MULT, op1=MAX)
-            elif RELU_ON[b * TILES + i] == "V":
-                nc.vector.tensor_scalar(out=res[:], in0=z[:], scalar1=0.15, scalar2=0.0, op0=MULT, op1=MAX)
+
+        def relu_and_store(i, b, engine):
+            row = rows[i, b][:]
+            if engine == "G":
+                nc.gpsimd.tensor_scalar(out=row, in0=row, scalar1=0.15, scalar2=0.0, op0=MULT, op1=MAX)
             else:
-                nc.scalar.activation(out=res[:], in_=z[:], func=RELU, scale=0.15)
-            nc.sync.dma_start(out=out[i * P : (i + 1) * P, cols], in_=res[:])
+                nc.scalar.activation(out=row, in_=row, func=RELU, scale=0.15)
+            nc.sync.dma_start(out=out_hbm[:, i, b * HALF : (b + 1) * HALF], in_=row)
 
-        def fill(m):
-            for k, step in enumerate(QUANT_H1):
-                if step == m:
-                    quant_h(k, 1)
-            for k, step in enumerate(QUANT_W):
-                if step == m:
-                    quant_w(k % 2, k // 2)
-            for k, (step, engine) in enumerate(LATE_H):
-                if step == m:
-                    ab = (k // 4, 1)
-                    interleave(engine, h_grp[ab], h_raw[ab], (k % 4) * P, (k % 4 + 1) * P)
-            for k, step in enumerate(WIDEN):
-                if step == m:
-                    widen_w((k % 8) // 4, k // 8, k % 4)
-            for k, (step, engine) in enumerate(MIX_W):
-                if step == m:
-                    ab = ((k % 8) // 4, k // 8)
-                    interleave(engine, w_grp[ab], w_wide[ab], (k % 4) * P, (k % 4 + 1) * P)
+        tasks = {}
+        tile_of = {}
+        i = 0
 
-        last = 2 * TILES
-        for m in range(-PT_LEAD, last + 10):
-            if 0 <= m + 1 < last:
-                matmul1(m + 1)
-            if 0 <= m < last:
-                make_q(m)
-                if FORM[m] == "T":
-                    transpose_q(m)
-                elif FORM[m] == "G":
-                    make_sg_row(m)
-            if 0 <= m - 1 < last and FORM[m - 1] == "G":
-                transpose_sg(m - 1)
-                copy_sg(m - 1)
-            if 0 <= m + PT_LEAD < TILES:
-                transpose_p(m + PT_LEAD)
-                copy_p(m + PT_LEAD)
-            if 0 <= m + 2 < TILES:
-                quant_p(m + 2)
-            if m == -4:
-                interleave("S", h_grp[0, 0], h_raw[0, 0], 0, S_SHARE)
-                interleave("V", h_grp[0, 0], h_raw[0, 0], S_SHARE, HALF)
-            if m == -3:
-                quant_h(0, 0)
-                interleave("S", h_grp[1, 0], h_raw[1, 0], 0, S_SHARE)
-                interleave("V", h_grp[1, 0], h_raw[1, 0], S_SHARE, HALF)
-            if m == -2:
-                quant_h(1, 0)
-            if 0 <= m - QS_LAG < last:
-                quant_s(m - QS_LAG)
-            if 0 <= m - 1 < last:
-                if FORM[m - 1] == "T":
-                    make_sg(m - 1)
-                elif FORM[m - 1] == "W":
-                    make_sg_row(m - 1)
-            if 0 <= m - 1 < last and FORM[m - 1] == "W":
-                transpose_sg(m - 1)
-                copy_sg(m - 1)
-            fill(m)
+        def add(name, engines, deps, emit, bank=False, frees=None):
+            tasks[name] = (engines, deps, emit, bank, frees)
+            tile_of[name] = i
+
+        arrive = {}
+        clock = HEAD
+        for name in LOADS:
+            clock += BYTES_OF[name[:2]]
+            arrive[name] = clock
+
+        def group_of(groups, i, letter):
+            for k, (lo, hi) in enumerate(groups):
+                if lo <= i < hi:
+                    return "%s%d" % (letter, k)
+
+        for a in range(2):
             for b in range(2):
-                i = m - MM2_STEP[b]
-                if 0 <= i < TILES and m <= last + 2:
-                    matmul2(i, b, "pt" if b else "tt")
-                i = m - MM2_STEP[b] - 1
-                if 0 <= i < TILES and m <= last + 2:
-                    finish(i, b)
-            if m == last + 2:
-                break
-        rest = [(i, b) for b in range(2) for i in range(TILES) if i + MM2_STEP[b] + 1 > last + 2]
-        pend = [x for x in rest if x[0] + MM2_STEP[x[1]] > last + 2]
-        tags = ["u", "tr", "pt", "tt"]
-        for k in range(min(3, len(pend))):
-            matmul2(pend[k][0], pend[k][1], tags[k % 4])
-        nxt = 3
-        for k, (i, b) in enumerate(rest):
-            finish(i, b)
-            if nxt < len(pend):
-                matmul2(pend[nxt][0], pend[nxt][1], tags[nxt % 4])
-                nxt += 1
+                for k in range(4):
+                    lo, hi = k * P, (k + 1) * P
+                    add(
+                        "hi%d%d%d" % (a, b, k),
+                        W["hi"],
+                        ["h%d0" % a],
+                        lambda e, n, a=a, b=b, lo=lo, hi=hi: interleave(e, h_grp[a, b], h_raw[a, b], lo, hi),
+                    )
+                    add(
+                        "wi%d%d%d" % (a, b, k),
+                        W["wi"],
+                        ["wd%d%d%d" % (a, b, t) for t in range(4)],
+                        lambda e, n, a=a, b=b, lo=lo, hi=hi: interleave(e, w_grp[a, b], w_wide[a, b][:], lo, hi),
+                    )
+                    add("wd%d%d%d" % (a, b, k), W["wd"], ["w%d" % a, "S"], lambda e, n, a=a, b=b, k=k: widen_w(a, b, k))
+                add("qh%d%d" % (a, b), W["qh"], ["hi%d%d%d" % (a, b, k) for k in range(4)], lambda e, n, a=a, b=b: quant_h(a, b))
+                add("qw%d%d" % (a, b), W["qw"], ["wi%d%d%d" % (a, b, k) for k in range(4)], lambda e, n, a=a, b=b: quant_w(a, b))
+        for i in range(TILES):
+            add("pt%d" % i, W["pt"], [group_of(P_GROUPS, i, "p")], lambda e, n, i=i: transpose_p(i, n), bank=True)
+            add("cp%d" % i, W["cp"], ["pt%d" % i], lambda e, n, i=i: copy_p(i, e), frees="pt%d" % i)
+            add("qp%d" % i, W["qp"], ["cp%d" % i], lambda e, n, i=i: quant_p(i))
+            done = []
+            for b in range(2):
+                m = 2 * i + b
+                ib = "%d%d" % (i, b)
+                add("m1" + ib, W["m1"], ["qp%d" % i, "qh0%d" % b, "qh1%d" % b], lambda e, n, m=m: matmul1(m, n), bank=True)
+                add("q" + ib, W["q"], ["m1" + ib, group_of(H0_GROUPS, i, "r")], lambda e, n, m=m: make_q(m), frees="m1" + ib)
+                if FORM[m] == "G":
+                    add("gg" + ib, W["gg"], ["q" + ib, "GR"], lambda e, n, m=m: gain_on_gpsimd(m))
+                    add("ts" + ib, W["ts"], ["gg" + ib], lambda e, n, m=m: transpose_sg(m, n), bank=True)
+                    add("cs" + ib, W["cs"], ["ts" + ib], lambda e, n, m=m: copy_sg(m), frees="ts" + ib)
+                    done.append("cs" + ib)
+                else:
+                    add("tr" + ib, W["tr"], ["q" + ib], lambda e, n, m=m: transpose_q(m, n), bank=True)
+                    add("sg" + ib, W["sg"], ["tr" + ib, "S"], lambda e, n, m=m: make_sg(m), frees="tr" + ib)
+                    done.append("sg" + ib)
+            add("qs%d" % i, W["qs"], done, lambda e, n, i=i: quant_s(i))
+            for b in range(2):
+                ib = "%d%d" % (i, b)
+                add("m2" + ib, W["m2"], ["qs%d" % i, "qw0%d" % b, "qw1%d" % b], lambda e, n, i=i, b=b: matmul2(i, b, n), bank=True)
+                add("z" + ib, W["z"], ["m2" + ib], lambda e, n, i=i, b=b: make_z(i, b), frees="m2" + ib)
+                add("re" + ib, W["re"], ["z" + ib], lambda e, n, i=i, b=b: relu_and_store(i, b, e))
+
+        users = {name: [] for name in list(tasks) + list(arrive)}
+        for name in tasks:
+            for dep in tasks[name][1]:
+                users[dep].append(name)
+        path = {}
+
+        def longest(name):
+            if name not in path:
+                cost = max(tasks[name][0].values()) + WAIT
+                path[name] = cost + max([longest(x) for x in users[name]] + [0])
+            return path[name]
+
+        rank = {name: longest(name) + BIAS.get([f for f in FAMILIES if name.startswith(f)][0], 0) - TILE_BIAS * tile_of[name] for name in tasks}
+        missing = {name: len([x for x in tasks[name][1] if x in tasks]) for name in tasks}
+        ready = [name for name in tasks if missing[name] == 0]
+        free = {"V": 0, "S": 0, "T": 0, "G": 0}
+        seen = {name: (arrive[name], "D") for name in arrive}
+        banks = [0] * 8
+        held = {}
+        port = 0
+        lastk = None
+        count = 0
+        while ready:
+            best = None
+            for engine in free:
+                options = []
+                for name in ready:
+                    engines, deps, emit, bank, frees = tasks[name]
+                    if engine not in engines or (bank and min(banks) >= NEVER):
+                        continue
+                    start = free[engine]
+                    for dep in deps:
+                        at, by = seen[dep]
+                        start = max(start, at if by == engine and engine != "V" else at + (0 if by == "D" else WAIT))
+                    if bank:
+                        start = max(start, min(banks))
+                    if engine == "G":
+                        start = max(start, port)
+                    options.append((start, name))
+                if not options:
+                    continue
+                soon = min(options)[0] + WINDOW[engine]
+                pick = max(
+                    (rank[name] - (FLEX if engine == "V" and len(tasks[name][0]) > 1 else 0) + (KEEP if engine == "T" and lastk == name[0] else 0), -start, name, start)
+                    for start, name in options
+                    if start <= soon
+                )
+                if best is None or pick[3] < best[0]:
+                    best = (pick[3], engine, pick[2])
+            start, engine, name = best
+            engines, deps, emit, bank, frees = tasks[name]
+            ready.remove(name)
+            if engine == "T":
+                if lastk and lastk != name[0]:
+                    start += SWITCH
+                lastk = name[0]
+            if engine == "G" or (engine == "V" and name[:2] in ("qp", "qh", "qs", "qw", "hi", "wi")):
+                start = max(start, port)
+                port = start + engines[engine]
+            free[engine] = start + engines[engine]
+            seen[name] = (free[engine], engine)
+            slot = None
+            if bank:
+                slot = min(range(8), key=lambda k: banks[k])
+                banks[slot] = NEVER
+                held[name] = slot
+            if frees:
+                banks[held[frees]] = free[engine] + WAIT
+            emit(engine, slot)
+            for x in users[name]:
+                missing[x] -= 1
+                if missing[x] == 0:
+                    ready.append(x)

from contextlib import ExitStack

import concourse.mybir as mybir
from concourse.masks import make_identity

N = 1024
FLOPS = 2 * 2 * N * N * N

F32 = mybir.dt.float32
BF16 = mybir.dt.bfloat16
U32 = mybir.dt.uint32
U8 = mybir.dt.uint8
FP8 = mybir.dt.float8_e4m3fn
FP8X4 = mybir.dt.float8_e4m3fn_x4
MULT = mybir.AluOpType.mult
ADD = mybir.AluOpType.add
MAX = mybir.AluOpType.max
COPY = mybir.ActivationFunctionType.Copy
RELU = mybir.ActivationFunctionType.Relu

P = 128
TILES = N // P
HALF = 512
P_GROUPS = ((0, 1), (1, 2), (2, 4), (4, 6), (6, 8))
H0_GROUPS = ((0, 2), (2, 4), (4, 6), (6, 8))
H_FULL = 'FF'
BYTES_OF = {'p0': 500, 'p1': 500, 'p2': 933, 'p3': 933, 'p4': 933, 'r0': 933, 'r1': 933, 'r2': 933, 'r3': 933, 'h0': 1790, 'h1': 1790, 'w0': 933, 'w1': 933, 'S': 800, 'GR': 500}
W = {'hi': {'V': 281, 'S': 515}, 'wi': {'V': 281, 'S': 515}, 'wd': {'S': 447}, 'qh': {'V': 463}, 'qw': {'V': 463}, 'pt': {'T': 424}, 'cp': {'V': 442, 'S': 447}, 'qp': {'V': 237}, 'm1': {'T': 440}, 'q': {'V': 442}, 'gg': {'G': 915}, 'ts': {'T': 212}, 'cs': {'S': 235}, 'tr': {'T': 424}, 'sg': {'V': 442}, 'qs': {'V': 237}, 'm2': {'T': 440}, 'z': {'V': 442}, 're': {'S': 447}}
LOADS = ('h10', 'h00', 'p0', 'p2', 'p1', 'w1', 'r0', 'S', 'r1', 'r2', 'p3', 'p4', 'w0', 'r3')
FORM = 'TTTTTTTTTTTTTTTT'
FAMILIES = ("hi", "wi", "wd", "qh", "qw", "pt", "cp", "qp", "gg", "ts", "cs", "tr", "sg", "qs", "re", "m", "q", "z")
BIAS = {'z': -500, 'gg': 18500, 'tr': 500, 'hi': 0, 'cs': -1500, 're': 6000, 'wi': -4500, 'qh': 3500, 'sg': 500, 'qp': -4000, 'q': 7500, 'qs': 9000, 'ts': -12500, 'cp': 4500, 'pt': -15500, 'm': 11000, 'qw': 7000, 'wd': -1000}
TILE_BIAS = 1000
FLEX = 10000
KEEP = 2000
WAIT = 180
SWITCH = 95
HEAD = 1500
NEVER = 1000000000
WINDOW = {'V': 0, 'S': 50, 'T': 0, 'G': 0}
OUT_BUFS = 8


def tile_gcniiinitialresidualidentitymap_kernel(tc, p, h, h0, g, w_bytes, w_scale, out):
    nc = tc.nc
    with ExitStack() as ctx:
        keep = ctx.enter_context(tc.tile_pool(name="keep", bufs=1))
        work = ctx.enter_context(tc.tile_pool(name="work", bufs=2))
        outs = ctx.enter_context(tc.tile_pool(name="outs", bufs=OUT_BUFS))
        psum = ctx.enter_context(tc.psum_pool(name="psum", bufs=1))
        ctx.enter_context(tc.manual_schedule())

        def kept(name, shape, dtype, tag=None):
            return keep.tile(shape, dtype, name=name, tag=tag or name, align_bytes=256)

        ident = kept("ident", [P, P], F32)
        g_bf = kept("g_bf", [P, 2, 4], BF16)
        gain = kept("gain", [P, 2, 4], F32)
        if "G" in FORM:
            g_row = kept("g_row", [P, N], BF16)
            gain_row = kept("gain_row", [P, N], F32)
        wsc = kept("wsc", [P, 2, 4], F32)
        warm = kept("warm", [P, 8], F32)
        p_raw, p_tile = {}, {}
        h0_raw, h0_tile = {}, {}
        for name, groups, rows, tiles in (("p_raw", P_GROUPS, p_raw, p_tile), ("h0_raw", H0_GROUPS, h0_raw, h0_tile)):
            for lo, hi in groups:
                tiles[lo] = kept("%s%d" % (name, lo), [P, hi - lo, N], BF16)
                for i in range(lo, hi):
                    rows[i] = tiles[lo][:, i - lo, :]
        p_codes = [kept("p_codes%d" % i, [P, 2, P], U32) for i in range(TILES)]
        p_scales = [kept("p_scales%d" % i, [P, 2, P], U8) for i in range(TILES)]
        q = [kept("q%d" % i, [P, N], F32) for i in range(TILES)]
        pairs = [(a, b) for a in range(2) for b in range(2)]
        h_raw = {}
        h_whole = {}
        for a in range(2):
            if H_FULL[a] == "F":
                h_whole[a] = kept("h_raw%d" % a, [P, 4, N], BF16)
                for b in range(2):
                    h_raw[a, b] = h_whole[a][:, :, b * HALF : (b + 1) * HALF]
            else:
                for b in range(2):
                    h_raw[a, b] = kept("h_raw%d%d" % (a, b), [P, 4, HALF], BF16)[:]
        h_grp = {ab: kept("h_grp%d%d" % ab, [P, HALF, 4], BF16) for ab in pairs}
        h_codes = {ab: kept("h_codes%d%d" % ab, [P, HALF], U32) for ab in pairs}
        h_scales = {ab: kept("h_scales%d%d" % ab, [P, HALF], U8) for ab in pairs}
        w_raw = [kept("w_raw%d" % a, [P, 4, N], U8) for a in range(2)]
        w_wide = {}
        w_grp = {ab: kept("w_grp%d%d" % ab, [P, HALF, 4], BF16) for ab in pairs}
        w_codes = {ab: kept("w_codes%d%d" % ab, [P, HALF], U32) for ab in pairs}
        w_scales = {ab: kept("w_scales%d%d" % ab, [P, HALF], U8) for ab in pairs}
        s_codes = [kept("s_codes%d" % i, [P, 2, P], U32) for i in range(TILES)]
        s_scales = [kept("s_scales%d" % i, [P, 2, P], U8) for i in range(TILES)]

        h_hbm = h.rearrange("(a p t) d -> a p t d", p=P, t=4)
        w_hbm = w_bytes.rearrange("(a p t) e -> a p t e", p=P, t=4)

        p_hbm = p.rearrange("(r i) k -> r i k", i=TILES)
        h0_hbm = h0.rearrange("(r i) d -> r i d", i=TILES)
        out_hbm = out.rearrange("(r i) e -> r i e", i=TILES)

        def load_p(k):
            lo, hi = P_GROUPS[k]
            nc.sync.dma_start(out=p_tile[lo][:], in_=p_hbm[:, lo:hi, :])

        def load_h0(k):
            lo, hi = H0_GROUPS[k]
            nc.sync.dma_start(out=h0_tile[lo][:], in_=h0_hbm[:, lo:hi, :])

        def load_h(a, b):
            if H_FULL[a] == "F":
                if b == 0:
                    nc.sync.dma_start(out=h_whole[a][:], in_=h_hbm[a])
            else:
                nc.sync.dma_start(out=h_raw[a, b], in_=h_hbm[a][:, :, b * HALF : (b + 1) * HALF])

        def load_w(a):
            nc.sync.dma_start(out=w_raw[a][:], in_=w_hbm[a])

        load_h(1, 0)
        load_h(0, 0)
        load_p(0)
        load_p(2)
        load_p(1)
        load_w(1)
        load_h0(0)
        nc.sync.dma_start(out=g_bf[:], in_=g.rearrange("(a p t) -> p a t", p=P, t=4))
        nc.sync.dma_start(out=wsc[:], in_=w_scale.rearrange("(a p t) o -> p a (t o)", p=P, t=4))
        load_h0(1)
        load_h0(2)
        load_p(3)
        load_p(4)
        load_w(0)
        load_h0(3)

        make_identity(nc, ident[:])
        nc.gpsimd.tensor_scalar(out=gain[:], in0=g_bf[:], scalar1=0.3, scalar2=0.0, op0=MULT, op1=ADD)
        if "G" in FORM:
            nc.gpsimd.tensor_scalar(out=gain_row[:], in0=g_row[:], scalar1=0.3, scalar2=0.0, op0=MULT, op1=ADD)
        nc.vector.memset(warm[:], 0.0)
        nc.scalar.activation(out=warm[:], in_=warm[:], func=RELU, scale=1.0)

        def interleave(engine, grouped, raw, lo, hi):
            dst = grouped[:, lo:hi, :]
            src = raw[:, :, lo:hi].rearrange("p t d -> p d t")
            if engine == "V":
                nc.vector.tensor_copy(out=dst, in_=src)
            elif engine == "S":
                nc.scalar.copy(out=dst, in_=src)
            else:
                nc.gpsimd.tensor_scalar(out=dst, in0=src, scalar1=1.0, scalar2=0.0, op0=MULT, op1=ADD)

        def widen_w(a, b, t):
            if (a, b) not in w_wide:
                w_wide[a, b] = kept("w_wide%d%d" % (a, b), [P, 4, HALF], BF16, tag=None if "F" in H_FULL else "h_raw%d%d" % (a, b))
            nc.scalar.activation(
                out=w_wide[a, b][:, t, :],
                in_=w_raw[a][:, t, b * HALF : (b + 1) * HALF].bitcast(FP8),
                func=COPY,
                scale=wsc[:, a, t : t + 1],
            )

        def quantize(codes, scales, grouped):
            nc.vector.quantize_mx(out=codes.bitcast(FP8X4), scales=scales, in_=grouped)

        def quant_h(a, b):
            quantize(h_codes[a, b][:], h_scales[a, b][:], h_grp[a, b][:].rearrange("p d t -> p (d t)"))

        def quant_w(a, b):
            quantize(w_codes[a, b][:], w_scales[a, b][:], w_grp[a, b][:].rearrange("p d t -> p (d t)"))

        pt = {}
        p_grp = {}
        u = {}
        tr = {}
        s_grp = {}
        tt = {}

        def transpose_p(i, bank):
            pt[i] = psum.tile([P, 2, 2, P], F32, name="pt", tag="bank%d" % bank)
            words = p_raw[i].bitcast(F32)
            for a in range(2):
                for half in range(2):
                    nc.tensor.transpose(pt[i][:, a, half, :], words[:, 256 * a + half : 256 * (a + 1) : 2], ident[:])

        def copy_p(i, engine):
            p_grp[i] = work.tile([P, 2, P, 4], BF16, name="p_grp", tag="p_grp", bufs=4, align_bytes=256)
            dst = p_grp[i][:].rearrange("p a r t -> p (a r t)").bitcast(F32).rearrange("p (a r u) -> p a r u", a=2, u=2)
            src = pt[i][:].rearrange("p a u r -> p a r u")
            if engine == "V":
                nc.vector.tensor_copy(out=dst, in_=src)
            else:
                nc.scalar.copy(out=dst, in_=src)

        def quant_p(i):
            quantize(
                p_codes[i][:].rearrange("p a r -> p (a r)"),
                p_scales[i][:].rearrange("p a r -> p (a r)"),
                p_grp[i][:].rearrange("p a r t -> p (a r t)"),
            )

        def matmul1(m, bank):
            i, b = divmod(m, 2)
            u[m] = psum.tile([P, HALF], F32, name="u", tag="bank%d" % bank)
            for a in range(2):
                nc.tensor.matmul_mx(
                    out=u[m][:],
                    lhsT=p_codes[i][:, a, :].bitcast(FP8X4),
                    lhsT_scale=p_scales[i][:, a, :],
                    rhs=h_codes[a, b][:].bitcast(FP8X4),
                    rhs_scale=h_scales[a, b][:],
                    start=(a == 0),
                    stop=(a == 1),
                )

        def make_q(m):
            i, b = divmod(m, 2)
            cols = slice(b * HALF, (b + 1) * HALF)
            nc.vector.scalar_tensor_tensor(
                out=q[i][:, cols], in0=u[m][:], scalar=7.0 / 3.0, in1=h0_raw[i][:, cols], op0=MULT, op1=ADD
            )

        def transpose_q(m, bank):
            i, b = divmod(m, 2)
            tr[m] = psum.tile([P, 4, P], F32, name="tr", tag="bank%d" % bank)
            for t in range(4):
                nc.tensor.transpose(tr[m][:, t, :], q[i][:, b * HALF + t : (b + 1) * HALF : 4], ident[:])

        sg = {}

        def s_group(i):
            if i not in s_grp:
                s_grp[i] = work.tile([P, 2, P, 4], BF16, name="s_grp", tag="s_grp", bufs=4, align_bytes=256)
            return s_grp[i]

        def gain_on_gpsimd(m):
            i, b = divmod(m, 2)
            cols = slice(b * HALF, (b + 1) * HALF)
            sg[m] = work.tile([P, HALF], BF16, name="sg", tag="sg", bufs=3, align_bytes=256)
            nc.gpsimd.tensor_tensor(out=sg[m][:], in0=q[i][:, cols], in1=gain_row[:, cols], op=MULT)

        def transpose_sg(m, bank):
            tr[m] = psum.tile([P, 2, P], F32, name="tr", tag="bank%d" % bank)
            words = sg[m][:].bitcast(F32)
            for half in range(2):
                nc.tensor.transpose(tr[m][:, half, :], words[:, half::2], ident[:])

        def copy_sg(m):
            i, b = divmod(m, 2)
            nc.scalar.copy(
                out=s_group(i)[:, b].rearrange("p r t -> p (r t)").bitcast(F32).rearrange("p (r u) -> p r u", u=2),
                in_=tr[m][:].rearrange("p u r -> p r u"),
            )

        def make_sg(m):
            i, b = divmod(m, 2)
            s_group(i)
            nc.vector.tensor_tensor(
                out=s_grp[i][:, b],
                in0=tr[m][:].rearrange("p t r -> p r t"),
                in1=gain[:, b, :].unsqueeze(1).to_broadcast([P, P, 4]),
                op=MULT,
            )

        def quant_s(i):
            quantize(
                s_codes[i][:].rearrange("p a r -> p (a r)"),
                s_scales[i][:].rearrange("p a r -> p (a r)"),
                s_grp[i][:].rearrange("p a r t -> p (a r t)"),
            )

        def matmul2(i, b, bank):
            tt[i, b] = psum.tile([P, HALF], F32, name="tt", tag="bank%d" % bank)
            for a in range(2):
                nc.tensor.matmul_mx(
                    out=tt[i, b][:],
                    lhsT=s_codes[i][:, a, :].bitcast(FP8X4),
                    lhsT_scale=s_scales[i][:, a, :],
                    rhs=w_codes[a, b][:].bitcast(FP8X4),
                    rhs_scale=w_scales[a, b][:],
                    start=(a == 0),
                    stop=(a == 1),
                )

        rows = {}

        def make_z(i, b):
            rows[i, b] = outs.tile([P, HALF], F32, name="row", tag="row")
            nc.vector.scalar_tensor_tensor(
                out=rows[i, b][:],
                in0=tt[i, b][:],
                scalar=10.0 / 3.0,
                in1=q[i][:, b * HALF : (b + 1) * HALF],
                op0=MULT,
                op1=ADD,
            )

        def relu_and_store(i, b, engine):
            row = rows[i, b][:]
            if engine == "G":
                nc.gpsimd.tensor_scalar(out=row, in0=row, scalar1=0.15, scalar2=0.0, op0=MULT, op1=MAX)
            else:
                nc.scalar.activation(out=row, in_=row, func=RELU, scale=0.15)
            nc.sync.dma_start(out=out_hbm[:, i, b * HALF : (b + 1) * HALF], in_=row)

        tasks = {}
        tile_of = {}
        i = 0

        def add(name, engines, deps, emit, bank=False, frees=None):
            tasks[name] = (engines, deps, emit, bank, frees)
            tile_of[name] = i

        arrive = {}
        clock = HEAD
        for name in LOADS:
            clock += BYTES_OF[name[:2]]
            arrive[name] = clock

        def group_of(groups, i, letter):
            for k, (lo, hi) in enumerate(groups):
                if lo <= i < hi:
                    return "%s%d" % (letter, k)

        for a in range(2):
            for b in range(2):
                for k in range(4):
                    lo, hi = k * P, (k + 1) * P
                    add(
                        "hi%d%d%d" % (a, b, k),
                        W["hi"],
                        ["h%d0" % a],
                        lambda e, n, a=a, b=b, lo=lo, hi=hi: interleave(e, h_grp[a, b], h_raw[a, b], lo, hi),
                    )
                    add(
                        "wi%d%d%d" % (a, b, k),
                        W["wi"],
                        ["wd%d%d%d" % (a, b, t) for t in range(4)],
                        lambda e, n, a=a, b=b, lo=lo, hi=hi: interleave(e, w_grp[a, b], w_wide[a, b][:], lo, hi),
                    )
                    add("wd%d%d%d" % (a, b, k), W["wd"], ["w%d" % a, "S"], lambda e, n, a=a, b=b, k=k: widen_w(a, b, k))
                add("qh%d%d" % (a, b), W["qh"], ["hi%d%d%d" % (a, b, k) for k in range(4)], lambda e, n, a=a, b=b: quant_h(a, b))
                add("qw%d%d" % (a, b), W["qw"], ["wi%d%d%d" % (a, b, k) for k in range(4)], lambda e, n, a=a, b=b: quant_w(a, b))
        for i in range(TILES):
            add("pt%d" % i, W["pt"], [group_of(P_GROUPS, i, "p")], lambda e, n, i=i: transpose_p(i, n), bank=True)
            add("cp%d" % i, W["cp"], ["pt%d" % i], lambda e, n, i=i: copy_p(i, e), frees="pt%d" % i)
            add("qp%d" % i, W["qp"], ["cp%d" % i], lambda e, n, i=i: quant_p(i))
            done = []
            for b in range(2):
                m = 2 * i + b
                ib = "%d%d" % (i, b)
                add("m1" + ib, W["m1"], ["qp%d" % i, "qh0%d" % b, "qh1%d" % b], lambda e, n, m=m: matmul1(m, n), bank=True)
                add("q" + ib, W["q"], ["m1" + ib, group_of(H0_GROUPS, i, "r")], lambda e, n, m=m: make_q(m), frees="m1" + ib)
                if FORM[m] == "G":
                    add("gg" + ib, W["gg"], ["q" + ib, "GR"], lambda e, n, m=m: gain_on_gpsimd(m))
                    add("ts" + ib, W["ts"], ["gg" + ib], lambda e, n, m=m: transpose_sg(m, n), bank=True)
                    add("cs" + ib, W["cs"], ["ts" + ib], lambda e, n, m=m: copy_sg(m), frees="ts" + ib)
                    done.append("cs" + ib)
                else:
                    add("tr" + ib, W["tr"], ["q" + ib], lambda e, n, m=m: transpose_q(m, n), bank=True)
                    add("sg" + ib, W["sg"], ["tr" + ib, "S"], lambda e, n, m=m: make_sg(m), frees="tr" + ib)
                    done.append("sg" + ib)
            add("qs%d" % i, W["qs"], done, lambda e, n, i=i: quant_s(i))
            for b in range(2):
                ib = "%d%d" % (i, b)
                add("m2" + ib, W["m2"], ["qs%d" % i, "qw0%d" % b, "qw1%d" % b], lambda e, n, i=i, b=b: matmul2(i, b, n), bank=True)
                add("z" + ib, W["z"], ["m2" + ib], lambda e, n, i=i, b=b: make_z(i, b), frees="m2" + ib)
                add("re" + ib, W["re"], ["z" + ib], lambda e, n, i=i, b=b: relu_and_store(i, b, e))

        users = {name: [] for name in list(tasks) + list(arrive)}
        for name in tasks:
            for dep in tasks[name][1]:
                users[dep].append(name)
        path = {}

        def longest(name):
            if name not in path:
                cost = max(tasks[name][0].values()) + WAIT
                path[name] = cost + max([longest(x) for x in users[name]] + [0])
            return path[name]

        rank = {name: longest(name) + BIAS.get([f for f in FAMILIES if name.startswith(f)][0], 0) - TILE_BIAS * tile_of[name] for name in tasks}
        missing = {name: len([x for x in tasks[name][1] if x in tasks]) for name in tasks}
        ready = [name for name in tasks if missing[name] == 0]
        free = {"V": 0, "S": 0, "T": 0, "G": 0}
        seen = {name: (arrive[name], "D") for name in arrive}
        banks = [0] * 8
        held = {}
        port = 0
        lastk = None
        count = 0
        while ready:
            best = None
            for engine in free:
                options = []
                for name in ready:
                    engines, deps, emit, bank, frees = tasks[name]
                    if engine not in engines or (bank and min(banks) >= NEVER):
                        continue
                    start = free[engine]
                    for dep in deps:
                        at, by = seen[dep]
                        start = max(start, at if by == engine and engine != "V" else at + (0 if by == "D" else WAIT))
                    if bank:
                        start = max(start, min(banks))
                    if engine == "G":
                        start = max(start, port)
                    options.append((start, name))
                if not options:
                    continue
                soon = min(options)[0] + WINDOW[engine]
                pick = max(
                    (rank[name] - (FLEX if engine == "V" and len(tasks[name][0]) > 1 else 0) + (KEEP if engine == "T" and lastk == name[0] else 0), -start, name, start)
                    for start, name in options
                    if start <= soon
                )
                if best is None or pick[3] < best[0]:
                    best = (pick[3], engine, pick[2])
            start, engine, name = best
            engines, deps, emit, bank, frees = tasks[name]
            ready.remove(name)
            if engine == "T":
                if lastk and lastk != name[0]:
                    start += SWITCH
                lastk = name[0]
            if engine == "G" or (engine == "V" and name[:2] in ("qp", "qh", "qs", "qw", "hi", "wi")):
                start = max(start, port)
                port = start + engines[engine]
            free[engine] = start + engines[engine]
            seen[name] = (free[engine], engine)
            slot = None
            if bank:
                slot = min(range(8), key=lambda k: banks[k])
                banks[slot] = NEVER
                held[name] = slot
            if frees:
                banks[held[frees]] = free[engine] + WAIT
            emit(engine, slot)
            for x in users[name]:
                missing[x] -= 1
                if missing[x] == 0:
                    ready.append(x)
